import numpy as np, ml_dtypes
CORES = [56,61,80,85]
N = 4
R, TK = 32, 128
def setup_inputs(rng):
    u = (rng.standard_normal((N, 128, R), dtype=np.float32) / 11).astype(ml_dtypes.bfloat16)
    return {"x": rng.standard_normal((N, 128, TK), dtype=np.float32).astype(ml_dtypes.bfloat16), "u": u, "ut": u.transpose(0, 2, 1).copy(), "vt": rng.standard_normal((N, R, 128), dtype=np.float32).astype(ml_dtypes.bfloat16)}
def setup_inputs_big(rng):
    d = setup_inputs(rng)
    for k in ("x", "u", "ut", "vt"): d[k] = (d[k].astype(np.float32) * 1024.0).astype(d[k].dtype)
    return d
def setup_inputs_small(rng):
    d = setup_inputs(rng)
    for k in ("x", "u", "ut", "vt"): d[k] = (d[k].astype(np.float32) * (1 / 1024.0)).astype(d[k].dtype)
    return d
def setup_inputs_apart(rng):
    d = setup_inputs(rng)
    f = (10.0 ** rng.permutation(np.linspace(-1.5, 1.5, N))).astype(np.float32).reshape(N, 1, 1)
    for k in ("x", "u", "ut", "vt"): d[k] = (d[k].astype(np.float32) * f).astype(d[k].dtype)
    return d
def tie_inputs(x):
    x = dict(x)
    x["ut"] = x["u"].transpose(0, 2, 1).copy()
    return x
def reference(x, u, ut, vt):
    X, U, VT = x.astype(np.float64), u.astype(np.float64), vt.astype(np.float64)
    y = np.stack([sum(VT[j].T @ (U[j].T @ X[r]) for j in range(N)) for r in range(N)])
    return {"y": y.astype(ml_dtypes.bfloat16 if x.dtype != np.float64 else np.float64)}

@@ -1,0 +1,112 @@
+from concourse.bass import DstId, RemoteDMATransfer
+
+SCRATCH = {
+    "utb": ("sbuf", [128, 128], "bfloat16"),
+    "vtb": ("sbuf", [128, 128], "bfloat16"),
+    "xb": ("sbuf", [128, 128], "bfloat16"),
+    "a_own": ("sbuf", [128, 128], "bfloat16"),
+    "a_peer": ("sbuf", [128, 128], "bfloat16"),
+    "a_far": ("sbuf", [128, 128], "bfloat16"),
+    "in0": ("sbuf", [128, 128], "bfloat16"),
+    "in1": ("sbuf", [128, 128], "bfloat16"),
+    "yb": ("sbuf", [128, 128], "bfloat16"),
+    "pa": ("psum", [128, 512], "float32"),
+    "py": ("psum", [128, 512], "float32"),
+}
+SEMAPHORES = ["ld", "ldx", "mm1", "cp1", "sent", "peer", "far", "got", "mm2", "cp2", "st"]
+
+RANK_ENGINES = 8
+RELAY_ENGINES = 8
+
+
+def _engines(mask, start, step, count):
+    bits = [b for b in range(mask.bit_length()) if (mask >> b) & 1][start::step][:count]
+    return sum(1 << b for b in bits)
+
+
+def _count(mask):
+    return bin(mask).count("1")
+
+
+def _relays(T, topo):
+    cores = list(T.cores)
+    chips = sorted({topo.chip(c) for c in cores})
+    out = {}
+    for ch in chips:
+        free = [k for k in range(topo.CORES_PER_CHIP * topo.CHIPS) if topo.chip(k) == ch and k not in cores]
+        for d in cores:
+            if topo.chip(d) == ch:
+                continue
+            can = [k for k in free if topo.may_write(k, d)]
+            same = [k for k in can if topo.die(k) == topo.die(d)]
+            k = (same or can)[0]
+            free.remove(k)
+            out[(ch, d)] = k
+    return out
+
+
+def rank_program(g, core, T, topo):
+    cores = list(T.cores)
+    relays = _relays(T, topo)
+    here = topo.chip(core)
+    S = T.sem
+
+    if T.rank_of(core) is None:
+        mine = [d for (ch, d), k in relays.items() if k == core]
+        if not mine:
+            return
+        d = mine[0]
+        n_src = len([c for c in cores if topo.chip(c) == here])
+        rid, pid, _ = topo.addr(d)
+        m = _engines(topo.mask(core, d), 0, 1, RELAY_ENGINES)
+        g.wait_ge(S.got, n_src * RANK_ENGINES)
+        g.remote_dma_fused(
+            [RemoteDMATransfer(dst_ids=[DstId(rid=rid, pnc=pid)], dma_engine_mask=m, remote_sem=S.far,
+                               srcs=[T.in0[:], T.in1[:]], dsts=[T.a_far[:]], alu_op=1)],
+            local_sem=S.sent)
+        g.wait_ge(S.sent, _count(m))
+        return
+
+    local = [c for c in cores if topo.chip(c) == here]
+    slot = local.index(core)
+    peer = [c for c in local if c != core][0]
+    my_relays = [relays[(here, d)] for d in cores if topo.chip(d) != here]
+
+    g.sync.dma_start(T.utb[0:32, :], T.ut[:]).then_inc(S.ld, 16)
+    g.scalar.dma_start(T.vtb[0:32, :], T.vt[:]).then_inc(S.ld, 16)
+    g.sync.dma_start(T.xb[:], T.x[:]).then_inc(S.ldx, 16)
+
+    g.tensor.wait_ge(S.ld, 32)
+    g.tensor.matmul(T.pa[:, 0:128], T.utb[0:32, :], T.vtb[0:32, :], True, True).then_inc(S.mm1, 1)
+    g.vector.wait_ge(S.mm1, 1)
+    g.vector.tensor_copy(T.a_own[:], T.pa[:, 0:128]).then_inc(S.cp1, 1)
+
+    g.wait_ge(S.cp1, 1)
+    trs = []
+    sent = 0
+    for i, k in enumerate(my_relays):
+        rid, pid, _ = topo.addr(k)
+        m = _engines(topo.mask(core, k), i, len(my_relays), RANK_ENGINES)
+        sent += _count(m)
+        trs.append(RemoteDMATransfer(dst_ids=[DstId(rid=rid, pnc=pid)], dma_engine_mask=m, remote_sem=S.got,
+                                     src=T.a_own[:], dst=T["in%d" % slot][:]))
+    g.remote_dma_fused(trs, local_sem=S.sent)
+    rid, pid, _ = topo.addr(peer)
+    pm = _engines(topo.mask(core, peer), 0, 1, len(my_relays) * RANK_ENGINES)
+    sent += _count(pm)
+    g.remote_dma(out_ap=T.a_peer[:], in_ap=T.a_own[:], remote_sem=S.peer, local_sem=S.sent,
+                 pid=pid, routing_id=rid, dma_engine_mask=pm)
+
+    g.tensor.wait_ge(S.cp1, 1)
+    g.tensor.wait_ge(S.ldx, 16)
+    g.tensor.matmul(T.py[:, 0:128], T.a_own[:], T.xb[:], True, False)
+    g.tensor.wait_ge(S.peer, _count(pm))
+    g.tensor.matmul(T.py[:, 0:128], T.a_peer[:], T.xb[:], False, False)
+    g.tensor.wait_ge(S.far, RELAY_ENGINES)
+    g.tensor.matmul(T.py[:, 0:128], T.a_far[:], T.xb[:], False, True).then_inc(S.mm2, 1)
+    g.vector.wait_ge(S.mm2, 1)
+    g.vector.tensor_copy(T.yb[:], T.py[:, 0:128]).then_inc(S.cp2, 1)
+    g.sync.wait_ge(S.cp2, 1)
+    g.sync.dma_start(T.y[:], T.yb[:]).then_inc(S.st, 16)
+    g.sync.wait_ge(S.st, 16)
+    g.wait_ge(S.sent, sent)

@@ -1,22 +1,30 @@
 from concourse.bass import DstId, RemoteDMATransfer
 
 SCRATCH = {
+    "ub": ("sbuf", [128, 32], "bfloat16"),
+    "vpad": ("sbuf", [128, 128], "bfloat16"),
     "utb": ("sbuf", [128, 128], "bfloat16"),
-    "vtb": ("sbuf", [128, 128], "bfloat16"),
     "xb": ("sbuf", [128, 128], "bfloat16"),
     "a_own": ("sbuf", [128, 128], "bfloat16"),
     "a_peer": ("sbuf", [128, 128], "bfloat16"),
-    "a_far": ("sbuf", [128, 128], "bfloat16"),
+    "u_far": ("sbuf", [128, 64], "bfloat16"),
+    "v_far": ("sbuf", [128, 128], "bfloat16"),
+    "t_far": ("sbuf", [128, 128], "bfloat16"),
+    "ubuf": ("sbuf", [128, 64], "bfloat16"),
     "in0": ("sbuf", [128, 128], "bfloat16"),
     "in1": ("sbuf", [128, 128], "bfloat16"),
     "yb": ("sbuf", [128, 128], "bfloat16"),
     "pa": ("psum", [128, 512], "float32"),
+    "pt": ("psum", [128, 512], "float32"),
     "py": ("psum", [128, 512], "float32"),
 }
-SEMAPHORES = ["ld", "ldx", "mm1", "cp1", "sent", "peer", "far", "got", "mm2", "cp2", "st"]
+SEMAPHORES = ["ldu", "ldv", "ldt", "ldx", "ms", "mm1", "cp1", "sent", "peer", "faru", "farv", "gotu", "gotv",
+              "mmt", "cpt", "mm2", "cp2", "st"]
 
-RANK_ENGINES = 8
+U_ENGINES = 4
+V_ENGINES = 8
 RELAY_ENGINES = 8
+R = 32
 
 
 def _engines(mask, start, step, count):
@@ -59,40 +67,59 @@ def rank_program(g, core, T, topo):
         n_src = len([c for c in cores if topo.chip(c) == here])
         rid, pid, _ = topo.addr(d)
         m = _engines(topo.mask(core, d), 0, 1, RELAY_ENGINES)
-        g.wait_ge(S.got, n_src * RANK_ENGINES)
+        g.wait_ge(S.gotu, n_src * U_ENGINES)
+        g.remote_dma(out_ap=T.u_far[:], in_ap=T.ubuf[:], remote_sem=S.faru, local_sem=S.sent,
+                     pid=pid, routing_id=rid, dma_engine_mask=m)
+        g.wait_ge(S.gotv, n_src * V_ENGINES)
         g.remote_dma_fused(
-            [RemoteDMATransfer(dst_ids=[DstId(rid=rid, pnc=pid)], dma_engine_mask=m, remote_sem=S.far,
-                               srcs=[T.in0[:], T.in1[:]], dsts=[T.a_far[:]], alu_op=1)],
+            [RemoteDMATransfer(dst_ids=[DstId(rid=rid, pnc=pid)], dma_engine_mask=m, remote_sem=S.farv,
+                               srcs=[T.in0[:], T.in1[:]], dsts=[T.v_far[:]], alu_op=1)],
             local_sem=S.sent)
-        g.wait_ge(S.sent, _count(m))
+        g.wait_ge(S.sent, 2 * _count(m))
         return
 
     local = [c for c in cores if topo.chip(c) == here]
     slot = local.index(core)
     peer = [c for c in local if c != core][0]
     my_relays = [relays[(here, d)] for d in cores if topo.chip(d) != here]
+    lo, hi = R * slot, R * slot + R
 
-    g.sync.dma_start(T.utb[0:32, :], T.ut[:]).then_inc(S.ld, 16)
-    g.scalar.dma_start(T.vtb[0:32, :], T.vt[:]).then_inc(S.ld, 16)
+    g.sync.dma_start(T.ub[:], T.u[:]).then_inc(S.ldu, 16)
+    g.scalar.dma_start(T.vpad[lo:hi, :], T.vt[:]).then_inc(S.ldv, 16)
+    g.scalar.dma_start(T.utb[lo:hi, :], T.ut[:]).then_inc(S.ldt, 16)
     g.sync.dma_start(T.xb[:], T.x[:]).then_inc(S.ldx, 16)
+    zero = [b for b in ((0, R), (R, 2 * R), (2 * R, 4 * R)) if b != (lo, hi)]
+    for a, b in zero:
+        g.vector.memset(T.vpad[a:b, :], 0.0).then_inc(S.ms, 1)
 
-    g.tensor.wait_ge(S.ld, 32)
-    g.tensor.matmul(T.pa[:, 0:128], T.utb[0:32, :], T.vtb[0:32, :], True, True).then_inc(S.mm1, 1)
+    sent = 0
+
+    def to_relays(src, dst, sem, n):
+        trs = []
+        tot = 0
+        for i, k in enumerate(my_relays):
+            rid, pid, _ = topo.addr(k)
+            m = _engines(topo.mask(core, k), i, len(my_relays), n)
+            tot += _count(m)
+            trs.append(RemoteDMATransfer(dst_ids=[DstId(rid=rid, pnc=pid)], dma_engine_mask=m, remote_sem=sem,
+                                         src=src, dst=dst))
+        g.remote_dma_fused(trs, local_sem=S.sent)
+        return tot
+
+    g.wait_ge(S.ldu, 16)
+    sent += to_relays(T.ub[:], T.ubuf[:, lo:hi], S.gotu, U_ENGINES)
+    g.wait_ge(S.ldv, 16)
+    g.wait_ge(S.ms, len(zero))
+    sent += to_relays(T.vpad[:], T["in%d" % slot][:], S.gotv, V_ENGINES)
+
+    g.tensor.wait_ge(S.ldv, 16)
+    g.tensor.wait_ge(S.ldt, 16)
+    g.tensor.matmul(T.pa[:, 0:128], T.utb[lo:hi, :], T.vpad[lo:hi, :], True, True).then_inc(S.mm1, 1)
     g.vector.wait_ge(S.mm1, 1)
     g.vector.tensor_copy(T.a_own[:], T.pa[:, 0:128]).then_inc(S.cp1, 1)
-
     g.wait_ge(S.cp1, 1)
-    trs = []
-    sent = 0
-    for i, k in enumerate(my_relays):
-        rid, pid, _ = topo.addr(k)
-        m = _engines(topo.mask(core, k), i, len(my_relays), RANK_ENGINES)
-        sent += _count(m)
-        trs.append(RemoteDMATransfer(dst_ids=[DstId(rid=rid, pnc=pid)], dma_engine_mask=m, remote_sem=S.got,
-                                     src=T.a_own[:], dst=T["in%d" % slot][:]))
-    g.remote_dma_fused(trs, local_sem=S.sent)
     rid, pid, _ = topo.addr(peer)
-    pm = _engines(topo.mask(core, peer), 0, 1, len(my_relays) * RANK_ENGINES)
+    pm = _engines(topo.mask(core, peer), 0, 1, len(my_relays) * max(U_ENGINES, V_ENGINES))
     sent += _count(pm)
     g.remote_dma(out_ap=T.a_peer[:], in_ap=T.a_own[:], remote_sem=S.peer, local_sem=S.sent,
                  pid=pid, routing_id=rid, dma_engine_mask=pm)
@@ -102,8 +129,13 @@ def rank_program(g, core, T, topo):
     g.tensor.matmul(T.py[:, 0:128], T.a_own[:], T.xb[:], True, False)
     g.tensor.wait_ge(S.peer, _count(pm))
     g.tensor.matmul(T.py[:, 0:128], T.a_peer[:], T.xb[:], False, False)
-    g.tensor.wait_ge(S.far, RELAY_ENGINES)
-    g.tensor.matmul(T.py[:, 0:128], T.a_far[:], T.xb[:], False, True).then_inc(S.mm2, 1)
+    g.tensor.wait_ge(S.faru, RELAY_ENGINES)
+    g.tensor.matmul(T.pt[0:64, 0:128], T.u_far[:], T.xb[:], True, True).then_inc(S.mmt, 1)
+    g.vector.wait_ge(S.mmt, 1)
+    g.vector.tensor_copy(T.t_far[0:64, :], T.pt[0:64, 0:128]).then_inc(S.cpt, 1)
+    g.tensor.wait_ge(S.cpt, 1)
+    g.tensor.wait_ge(S.farv, RELAY_ENGINES)
+    g.tensor.matmul(T.py[:, 0:128], T.v_far[0:64, :], T.t_far[0:64, :], False, True).then_inc(S.mm2, 1)
     g.vector.wait_ge(S.mm2, 1)
     g.vector.tensor_copy(T.yb[:], T.py[:, 0:128]).then_inc(S.cp2, 1)
     g.sync.wait_ge(S.cp2, 1)

@@ -1,18 +1,26 @@
 from concourse.bass import DstId, RemoteDMATransfer
 
+R = 32
+SPLIT = 2
+W = 128 // SPLIT
+U_ENGINES = 2
+V_ENGINES = 4
+RELAY_ENGINES = 8
+PEER_ENGINES = 16
+
 SCRATCH = {
-    "ub": ("sbuf", [128, 32], "bfloat16"),
+    "ud": ("dram", [128, R], "bfloat16"),
+    "ug": ("dram", [128, R], "bfloat16"),
     "vpad": ("sbuf", [128, 128], "bfloat16"),
     "utb": ("sbuf", [128, 128], "bfloat16"),
     "xb": ("sbuf", [128, 128], "bfloat16"),
     "a_own": ("sbuf", [128, 128], "bfloat16"),
     "a_peer": ("sbuf", [128, 128], "bfloat16"),
-    "u_far": ("sbuf", [128, 64], "bfloat16"),
+    "u_far": ("sbuf", [128, 2 * R], "bfloat16"),
     "v_far": ("sbuf", [128, 128], "bfloat16"),
     "t_far": ("sbuf", [128, 128], "bfloat16"),
-    "ubuf": ("sbuf", [128, 64], "bfloat16"),
-    "in0": ("sbuf", [128, 128], "bfloat16"),
-    "in1": ("sbuf", [128, 128], "bfloat16"),
+    "in0": ("sbuf", [128, W], "bfloat16"),
+    "in1": ("sbuf", [128, W], "bfloat16"),
     "yb": ("sbuf", [128, 128], "bfloat16"),
     "pa": ("psum", [128, 512], "float32"),
     "pt": ("psum", [128, 512], "float32"),
@@ -20,11 +28,6 @@ SCRATCH = {
 }
 SEMAPHORES = ["ldu", "ldv", "ldt", "ldx", "ms", "mm1", "cp1", "sent", "peer", "faru", "farv", "gotu", "gotv",
               "mmt", "cpt", "mm2", "cp2", "st"]
-
-U_ENGINES = 4
-V_ENGINES = 8
-RELAY_ENGINES = 8
-R = 32
 
 
 def _engines(mask, start, step, count):
@@ -42,14 +45,15 @@ def _relays(T, topo):
     out = {}
     for ch in chips:
         free = [k for k in range(topo.CORES_PER_CHIP * topo.CHIPS) if topo.chip(k) == ch and k not in cores]
-        for d in cores:
-            if topo.chip(d) == ch:
-                continue
-            can = [k for k in free if topo.may_write(k, d)]
-            same = [k for k in can if topo.die(k) == topo.die(d)]
-            k = (same or can)[0]
-            free.remove(k)
-            out[(ch, d)] = k
+        for h in range(SPLIT):
+            for d in cores:
+                if topo.chip(d) == ch:
+                    continue
+                can = [k for k in free if topo.may_write(k, d)]
+                same = [k for k in can if topo.die(k) == topo.die(d)]
+                k = (same or can)[0]
+                free.remove(k)
+                out[(ch, h, d)] = k
     return out
 
 
@@ -60,20 +64,20 @@ def rank_program(g, core, T, topo):
     S = T.sem
 
     if T.rank_of(core) is None:
-        mine = [d for (ch, d), k in relays.items() if k == core]
+        mine = [(h, d) for (ch, h, d), k in relays.items() if k == core]
         if not mine:
             return
-        d = mine[0]
+        h, d = mine[0]
         n_src = len([c for c in cores if topo.chip(c) == here])
         rid, pid, _ = topo.addr(d)
         m = _engines(topo.mask(core, d), 0, 1, RELAY_ENGINES)
-        g.wait_ge(S.gotu, n_src * U_ENGINES)
-        g.remote_dma(out_ap=T.u_far[:], in_ap=T.ubuf[:], remote_sem=S.faru, local_sem=S.sent,
+        g.wait_ge(S.gotu, U_ENGINES)
+        g.remote_dma(out_ap=T.u_far[:, h * R:(h + 1) * R], in_ap=T.ug[:], remote_sem=S.faru, local_sem=S.sent,
                      pid=pid, routing_id=rid, dma_engine_mask=m)
         g.wait_ge(S.gotv, n_src * V_ENGINES)
         g.remote_dma_fused(
             [RemoteDMATransfer(dst_ids=[DstId(rid=rid, pnc=pid)], dma_engine_mask=m, remote_sem=S.farv,
-                               srcs=[T.in0[:], T.in1[:]], dsts=[T.v_far[:]], alu_op=1)],
+                               srcs=[T.in0[:], T.in1[:]], dsts=[T.v_far[:, h * W:(h + 1) * W]], alu_op=1)],
             local_sem=S.sent)
         g.wait_ge(S.sent, 2 * _count(m))
         return
@@ -81,10 +85,10 @@ def rank_program(g, core, T, topo):
     local = [c for c in cores if topo.chip(c) == here]
     slot = local.index(core)
     peer = [c for c in local if c != core][0]
-    my_relays = [relays[(here, d)] for d in cores if topo.chip(d) != here]
+    my_relays = [(h, k) for (ch, h, d), k in relays.items() if ch == here]
     lo, hi = R * slot, R * slot + R
 
-    g.sync.dma_start(T.ub[:], T.u[:]).then_inc(S.ldu, 16)
+    g.sync.dma_start(T.ud[:], T.u[:]).then_inc(S.ldu, 16)
     g.scalar.dma_start(T.vpad[lo:hi, :], T.vt[:]).then_inc(S.ldv, 16)
     g.scalar.dma_start(T.utb[lo:hi, :], T.ut[:]).then_inc(S.ldt, 16)
     g.sync.dma_start(T.xb[:], T.x[:]).then_inc(S.ldx, 16)
@@ -92,14 +96,12 @@ def rank_program(g, core, T, topo):
     for a, b in zero:
         g.vector.memset(T.vpad[a:b, :], 0.0).then_inc(S.ms, 1)
 
-    sent = 0
-
-    def to_relays(src, dst, sem, n):
+    def to_relays(items, sem, n):
         trs = []
         tot = 0
-        for i, k in enumerate(my_relays):
+        for i, (k, src, dst) in enumerate(items):
             rid, pid, _ = topo.addr(k)
-            m = _engines(topo.mask(core, k), i, len(my_relays), n)
+            m = _engines(topo.mask(core, k), i, len(items), n)
             tot += _count(m)
             trs.append(RemoteDMATransfer(dst_ids=[DstId(rid=rid, pnc=pid)], dma_engine_mask=m, remote_sem=sem,
                                          src=src, dst=dst))
@@ -107,10 +109,11 @@ def rank_program(g, core, T, topo):
         return tot
 
     g.wait_ge(S.ldu, 16)
-    sent += to_relays(T.ub[:], T.ubuf[:, lo:hi], S.gotu, U_ENGINES)
+    sent = to_relays([(k, T.ud[:], T.ug[:]) for h, k in my_relays if h == slot], S.gotu, U_ENGINES)
     g.wait_ge(S.ldv, 16)
     g.wait_ge(S.ms, len(zero))
-    sent += to_relays(T.vpad[:], T["in%d" % slot][:], S.gotv, V_ENGINES)
+    sent += to_relays([(k, T.vpad[:, h * W:(h + 1) * W], T["in%d" % slot][:]) for h, k in my_relays],
+                      S.gotv, V_ENGINES)
 
     g.tensor.wait_ge(S.ldv, 16)
     g.tensor.wait_ge(S.ldt, 16)
@@ -119,7 +122,7 @@ def rank_program(g, core, T, topo):
     g.vector.tensor_copy(T.a_own[:], T.pa[:, 0:128]).then_inc(S.cp1, 1)
     g.wait_ge(S.cp1, 1)
     rid, pid, _ = topo.addr(peer)
-    pm = _engines(topo.mask(core, peer), 0, 1, len(my_relays) * max(U_ENGINES, V_ENGINES))
+    pm = _engines(topo.mask(core, peer), 0, 1, PEER_ENGINES)
     sent += _count(pm)
     g.remote_dma(out_ap=T.a_peer[:], in_ap=T.a_own[:], remote_sem=S.peer, local_sem=S.sent,
                  pid=pid, routing_id=rid, dma_engine_mask=pm)
@@ -129,12 +132,12 @@ def rank_program(g, core, T, topo):
     g.tensor.matmul(T.py[:, 0:128], T.a_own[:], T.xb[:], True, False)
     g.tensor.wait_ge(S.peer, _count(pm))
     g.tensor.matmul(T.py[:, 0:128], T.a_peer[:], T.xb[:], False, False)
-    g.tensor.wait_ge(S.faru, RELAY_ENGINES)
+    g.tensor.wait_ge(S.faru, SPLIT * RELAY_ENGINES)
     g.tensor.matmul(T.pt[0:64, 0:128], T.u_far[:], T.xb[:], True, True).then_inc(S.mmt, 1)
     g.vector.wait_ge(S.mmt, 1)
     g.vector.tensor_copy(T.t_far[0:64, :], T.pt[0:64, 0:128]).then_inc(S.cpt, 1)
     g.tensor.wait_ge(S.cpt, 1)
-    g.tensor.wait_ge(S.farv, RELAY_ENGINES)
+    g.tensor.wait_ge(S.farv, SPLIT * RELAY_ENGINES)
     g.tensor.matmul(T.py[:, 0:128], T.v_far[0:64, :], T.t_far[0:64, :], False, True).then_inc(S.mm2, 1)
     g.vector.wait_ge(S.mm2, 1)
     g.vector.tensor_copy(T.yb[:], T.py[:, 0:128]).then_inc(S.cp2, 1)

from concourse.bass import DstId, RemoteDMATransfer

R = 32
SPLIT = 2
W = 128 // SPLIT
U_ENGINES = 2
V_ENGINES = 4
RELAY_ENGINES = 8
PEER_ENGINES = 16

SCRATCH = {
    "ud": ("dram", [128, R], "bfloat16"),
    "ug": ("dram", [128, R], "bfloat16"),
    "vpad": ("sbuf", [128, 128], "bfloat16"),
    "utb": ("sbuf", [128, 128], "bfloat16"),
    "xb": ("sbuf", [128, 128], "bfloat16"),
    "a_own": ("sbuf", [128, 128], "bfloat16"),
    "a_peer": ("sbuf", [128, 128], "bfloat16"),
    "u_far": ("sbuf", [128, 2 * R], "bfloat16"),
    "v_far": ("sbuf", [128, 128], "bfloat16"),
    "t_far": ("sbuf", [128, 128], "bfloat16"),
    "in0": ("sbuf", [128, W], "bfloat16"),
    "in1": ("sbuf", [128, W], "bfloat16"),
    "yb": ("sbuf", [128, 128], "bfloat16"),
    "pa": ("psum", [128, 512], "float32"),
    "pt": ("psum", [128, 512], "float32"),
    "py": ("psum", [128, 512], "float32"),
}
SEMAPHORES = ["ldu", "ldv", "ldt", "ldx", "ms", "mm1", "cp1", "sent", "peer", "faru", "farv", "gotu", "gotv",
              "mmt", "cpt", "mm2", "cp2", "st"]


def _engines(mask, start, step, count):
    bits = [b for b in range(mask.bit_length()) if (mask >> b) & 1][start::step][:count]
    return sum(1 << b for b in bits)


def _count(mask):
    return bin(mask).count("1")


def _relays(T, topo):
    cores = list(T.cores)
    chips = sorted({topo.chip(c) for c in cores})
    out = {}
    for ch in chips:
        free = [k for k in range(topo.CORES_PER_CHIP * topo.CHIPS) if topo.chip(k) == ch and k not in cores]
        for h in range(SPLIT):
            for d in cores:
                if topo.chip(d) == ch:
                    continue
                can = [k for k in free if topo.may_write(k, d)]
                same = [k for k in can if topo.die(k) == topo.die(d)]
                k = (same or can)[0]
                free.remove(k)
                out[(ch, h, d)] = k
    return out


def rank_program(g, core, T, topo):
    cores = list(T.cores)
    relays = _relays(T, topo)
    here = topo.chip(core)
    S = T.sem

    if T.rank_of(core) is None:
        mine = [(h, d) for (ch, h, d), k in relays.items() if k == core]
        if not mine:
            return
        h, d = mine[0]
        n_src = len([c for c in cores if topo.chip(c) == here])
        rid, pid, _ = topo.addr(d)
        m = _engines(topo.mask(core, d), 0, 1, RELAY_ENGINES)
        g.wait_ge(S.gotu, U_ENGINES)
        g.remote_dma(out_ap=T.u_far[:, h * R:(h + 1) * R], in_ap=T.ug[:], remote_sem=S.faru, local_sem=S.sent,
                     pid=pid, routing_id=rid, dma_engine_mask=m)
        g.wait_ge(S.gotv, n_src * V_ENGINES)
        g.remote_dma_fused(
            [RemoteDMATransfer(dst_ids=[DstId(rid=rid, pnc=pid)], dma_engine_mask=m, remote_sem=S.farv,
                               srcs=[T.in0[:], T.in1[:]], dsts=[T.v_far[:, h * W:(h + 1) * W]], alu_op=1)],
            local_sem=S.sent)
        g.wait_ge(S.sent, 2 * _count(m))
        return

    local = [c for c in cores if topo.chip(c) == here]
    slot = local.index(core)
    peer = [c for c in local if c != core][0]
    my_relays = [(h, k) for (ch, h, d), k in relays.items() if ch == here]
    lo, hi = R * slot, R * slot + R

    g.sync.dma_start(T.ud[:], T.u[:]).then_inc(S.ldu, 16)
    g.scalar.dma_start(T.vpad[lo:hi, :], T.vt[:]).then_inc(S.ldv, 16)
    g.scalar.dma_start(T.utb[lo:hi, :], T.ut[:]).then_inc(S.ldt, 16)
    g.sync.dma_start(T.xb[:], T.x[:]).then_inc(S.ldx, 16)
    zero = [b for b in ((0, R), (R, 2 * R), (2 * R, 4 * R)) if b != (lo, hi)]
    for a, b in zero:
        g.vector.memset(T.vpad[a:b, :], 0.0).then_inc(S.ms, 1)

    def to_relays(items, sem, n):
        trs = []
        tot = 0
        for i, (k, src, dst) in enumerate(items):
            rid, pid, _ = topo.addr(k)
            m = _engines(topo.mask(core, k), i, len(items), n)
            tot += _count(m)
            trs.append(RemoteDMATransfer(dst_ids=[DstId(rid=rid, pnc=pid)], dma_engine_mask=m, remote_sem=sem,
                                         src=src, dst=dst))
        g.remote_dma_fused(trs, local_sem=S.sent)
        return tot

    g.wait_ge(S.ldu, 16)
    sent = to_relays([(k, T.ud[:], T.ug[:]) for h, k in my_relays if h == slot], S.gotu, U_ENGINES)
    g.wait_ge(S.ldv, 16)
    g.wait_ge(S.ms, len(zero))
    sent += to_relays([(k, T.vpad[:, h * W:(h + 1) * W], T["in%d" % slot][:]) for h, k in my_relays],
                      S.gotv, V_ENGINES)

    g.tensor.wait_ge(S.ldv, 16)
    g.tensor.wait_ge(S.ldt, 16)
    g.tensor.matmul(T.pa[:, 0:128], T.utb[lo:hi, :], T.vpad[lo:hi, :], True, True).then_inc(S.mm1, 1)
    g.vector.wait_ge(S.mm1, 1)
    g.vector.tensor_copy(T.a_own[:], T.pa[:, 0:128]).then_inc(S.cp1, 1)
    g.wait_ge(S.cp1, 1)
    rid, pid, _ = topo.addr(peer)
    pm = _engines(topo.mask(core, peer), 0, 1, PEER_ENGINES)
    sent += _count(pm)
    g.remote_dma(out_ap=T.a_peer[:], in_ap=T.a_own[:], remote_sem=S.peer, local_sem=S.sent,
                 pid=pid, routing_id=rid, dma_engine_mask=pm)

    g.tensor.wait_ge(S.cp1, 1)
    g.tensor.wait_ge(S.ldx, 16)
    g.tensor.matmul(T.py[:, 0:128], T.a_own[:], T.xb[:], True, False)
    g.tensor.wait_ge(S.peer, _count(pm))
    g.tensor.matmul(T.py[:, 0:128], T.a_peer[:], T.xb[:], False, False)
    g.tensor.wait_ge(S.faru, SPLIT * RELAY_ENGINES)
    g.tensor.matmul(T.pt[0:64, 0:128], T.u_far[:], T.xb[:], True, True).then_inc(S.mmt, 1)
    g.vector.wait_ge(S.mmt, 1)
    g.vector.tensor_copy(T.t_far[0:64, :], T.pt[0:64, 0:128]).then_inc(S.cpt, 1)
    g.tensor.wait_ge(S.cpt, 1)
    g.tensor.wait_ge(S.farv, SPLIT * RELAY_ENGINES)
    g.tensor.matmul(T.py[:, 0:128], T.v_far[0:64, :], T.t_far[0:64, :], False, True).then_inc(S.mm2, 1)
    g.vector.wait_ge(S.mm2, 1)
    g.vector.tensor_copy(T.yb[:], T.py[:, 0:128]).then_inc(S.cp2, 1)
    g.sync.wait_ge(S.cp2, 1)
    g.sync.dma_start(T.y[:], T.yb[:]).then_inc(S.st, 16)
    g.sync.wait_ge(S.st, 16)
    g.wait_ge(S.sent, sent)
